import numpy as np
import ml_dtypes


def mxq(x, axis, fmt="e4m3"):
    dtype, down = {"e4m3": (ml_dtypes.float8_e4m3fn, 7), "e5m2": (ml_dtypes.float8_e5m2, 14)}[fmt]
    v = np.moveaxis(np.asarray(x, np.float32).astype(ml_dtypes.bfloat16).astype(np.float64), axis, -1)
    blocks = v.reshape(v.shape[:-1] + (-1, 32))
    amax = np.abs(blocks).max(-1, keepdims=True)
    byte = np.maximum(np.where(amax > 0, np.frexp(amax)[1] - 1 + 127, 0) - down, 1)
    scale = np.exp2(byte - 127.0)
    codes = (blocks / scale).astype(np.float32).astype(dtype).astype(np.float64)
    return np.moveaxis((codes * scale).reshape(v.shape), -1, axis)


WIDE = False


def mx_kscale(k):
    if not WIDE:
        return np.ones(k)
    levels = np.array([10, -10, 5, -5, 0])
    if k % 512:
        return np.exp2(np.random.permutation(np.resize(levels, k // 32))).repeat(32)
    a = np.empty((k // 512, 16))
    for p in range(k // 512):
        a[p, :8] = np.random.permutation(np.resize(levels, 8))
        for g in range(8):
            far = levels[np.abs(levels - a[p, g]) >= 10]
            a[p, g + 8] = far[np.random.randint(len(far))]
    return np.exp2(a.ravel()).repeat(32)


def f64(x):
    return np.asarray(x).astype(np.float64)


def striped(idx):
    return np.tile(idx.reshape(-1, 16).T, (8, 1)).astype(np.uint16)


def unstriped(offs):
    return offs[:16].T.reshape(-1).astype(np.int64)


def pack_weight(w):
    k, n = w.shape
    w = f64(np.asarray(w, np.float32).astype(ml_dtypes.bfloat16)).reshape(k // 32, 32, n)
    amax = np.abs(w).max(1)
    byte = np.clip(np.where(amax > 0, np.frexp(amax)[1] - 1 + 127 - 7, 1), 1, 254)
    scaled = (w * np.exp2(127.0 - byte)[:, None, :]).reshape(k, n).astype(np.float32)
    words = np.ascontiguousarray(scaled.reshape(k // 512, 128, 4, n).transpose(0, 1, 3, 2)).astype(ml_dtypes.float8_e4m3fn).view(np.uint8)
    return words, np.ascontiguousarray(byte.astype(np.uint8).reshape(k // 512, 16, n))


def unpack_weight(words, scales):
    g, p, n, _ = words.shape
    vals = np.ascontiguousarray(words).view(ml_dtypes.float8_e4m3fn).astype(np.float64) * np.repeat(np.exp2(scales.astype(np.float64) - 127.0), 8, axis=1)[..., None]
    return vals.transpose(0, 1, 3, 2).reshape(g * 512, n)


def sigmoid(v):
    return 1.0 / (1.0 + np.exp(-np.maximum(v, -700.0)))


K, T, S, D, N, H, V, U = 1024, 2048, 1024, 4, 256, 512, 256, 512


def setup_inputs():
    n = np.random.standard_normal
    s = mx_kscale(K)[:, None]
    u = mx_kscale(H)
    packed_xT = pack_weight(n((K, T)) * s)
    return {
        "x_words": packed_xT[0],
        "x_scales": packed_xT[1],
        "w1": (n((K, H)) / np.sqrt(K) / s).astype(np.float32),
        "w2": (n((K, H)) / np.sqrt(K) / s).astype(np.float32),
        "unit": (np.random.uniform(0.6, 1.4, (H, 1)) * u[:, None]).astype(np.float32),
        "w3": (n((H, N)) / np.sqrt(H) / u[:, None]).astype(np.float32),
        "offs": striped(np.random.permutation(T)[:S]),
        "va": striped(np.random.permutation(np.concatenate([np.arange(V), np.random.randint(0, V, U - V)]))),
        "vb2": striped(np.random.permutation(np.concatenate([np.arange(V), np.random.randint(0, V, U - V)]))),
    }


def reference(x_words, x_scales, w1, w2, unit, w3, offs, va, vb2):
    xq = unpack_weight(x_words, x_scales)[:, unstriped(offs)]
    y = mxq(f64(w1), 0, "e4m3").T @ xq
    yv = mxq(f64(w2), 0, "e4m3").T @ xq
    visi = sigmoid(2.0 * yv)
    yl = y * visi
    direct = yl.reshape(len(yl), -1, D).sum(axis=2)
    la = direct[:, unstriped(va)]
    open_ = visi.reshape(len(visi), -1, D).mean(axis=2)
    aa = open_[:, unstriped(va)]
    lb = direct[:, unstriped(vb2)]
    bounce = la + 0.8 * ((-1.0 * aa + 1.0) * lb)
    hid = f64(unit) * bounce
    return mxq(f64(w3), 0, "e4m3").T @ mxq(hid, 0, "e4m3")

@@ -1,0 +1,221 @@
+from contextlib import ExitStack
+
+import concourse.mybir as mybir
+from concourse.masks import make_identity
+
+K, T, S, D, N, H, V, U = 1024, 2048, 1024, 4, 256, 512, 256, 512
+FLOPS = 2 * (2 * K * H * S + H * N * U)
+
+F32 = mybir.dt.float32
+BF16 = mybir.dt.bfloat16
+I32 = mybir.dt.int32
+U32 = mybir.dt.uint32
+U16 = mybir.dt.uint16
+U8 = mybir.dt.uint8
+FP8X4 = mybir.dt.float8_e4m3fn_x4
+ACT = mybir.ActivationFunctionType
+ALU = mybir.AluOpType
+
+P = 128
+PACK = 4
+K_PASS = P * PACK
+PASSES = K // K_PASS
+WINDOW = U + 16
+
+
+def tile_picked_yprtrn_lin_p_kernel(
+    tc, x_words, x_scales, w1, w2, unit, w3, offs, va, vb2, out
+):
+    nc = tc.nc
+    with ExitStack() as ctx:
+        keep = ctx.enter_context(tc.tile_pool(name="keep", bufs=1))
+        mm = ctx.enter_context(tc.psum_pool(name="mm", bufs=6))
+        acc = ctx.enter_context(tc.psum_pool(name="acc", bufs=2))
+
+        offs_sb = keep.tile([P, S // 16], U16, name="offs_sb")
+        va_sb = keep.tile([P, U // 16], U16, name="va_sb")
+        vb_sb = keep.tile([P, U // 16], U16, name="vb_sb")
+        x_planes = keep.tile([P, T], U8, name="x_planes")
+        nc.gpsimd.memset(x_planes[:].bitcast(I32), 0)
+        nc.sync.dma_start(offs_sb[:], offs)
+
+        x_table = [keep.tile([P, T], U32, name="x_table%d" % o) for o in range(PASSES)]
+        raw = {
+            (name, o): keep.tile([P, PACK, H], F32, name="raw_%s%d" % (name, o))
+            for name in ("w2", "w1")
+            for o in range(PASSES)
+        }
+        raw3 = keep.tile([P, PACK, N], F32, name="raw3")
+        unit_sb = keep.tile([P, PACK], F32, name="unit_sb")
+
+        def load_x(o):
+            nc.sync.dma_start(
+                x_table[o][:].bitcast(I32),
+                x_words[o].rearrange("p n t -> p (n t)").bitcast(I32),
+            )
+
+        def load_w(name, w, o):
+            rows = w[o * K_PASS : (o + 1) * K_PASS, :]
+            nc.sync.dma_start(raw[name, o][:], rows.rearrange("(p j) c -> p j c", j=PACK))
+
+        for q in range(4):
+            nc.sync.dma_start(
+                x_planes[32 * q : 32 * q + 8, :].bitcast(I32),
+                x_scales[:, 4 * q : 4 * q + 4, :].bitcast(I32),
+            )
+        load_x(0)
+        load_w("w2", w2, 0)
+        load_x(1)
+        load_w("w2", w2, 1)
+        load_w("w1", w1, 0)
+        load_w("w1", w1, 1)
+        nc.sync.dma_start(va_sb[:], va)
+        nc.sync.dma_start(vb_sb[:], vb2)
+        nc.sync.dma_start(unit_sb[:], unit.rearrange("(p t) o -> p (t o)", t=PACK))
+        nc.sync.dma_start(raw3[:], w3.rearrange("(p j) c -> p j c", j=PACK))
+
+        ident = keep.tile([P, P], F32, name="ident")
+        make_identity(nc, ident[:])
+
+        closed = [keep.tile([P, WINDOW], F32, name="closed%d" % t) for t in range(PACK)]
+        direct = [keep.tile([P, WINDOW], F32, name="direct%d" % t) for t in range(PACK)]
+        for table in closed + direct:
+            nc.gpsimd.memset(table[:, V:], 0.0)
+
+        def dealt(tile):
+            return tile[:].rearrange("p (h d v) -> p h v d", h=2, d=D)
+
+        xs = keep.tile([P, S], U8, name="xs", align_bytes=64)
+        xw = [keep.tile([P, S], U32, name="xw%d" % o, align_bytes=64) for o in range(PASSES)]
+
+        codes, planes = {}, {}
+
+        def interleave(name, o, v_cols):
+            grouped = keep.tile([P, PACK * H], BF16, name="grp_%s%d" % (name, o), align_bytes=64)
+            dst = grouped[:].rearrange("p (t m j) -> p m j t", t=PACK, j=PACK)
+            src = raw[name, o][:].rearrange("p j (m t) -> p m j t", t=PACK)
+            if v_cols > 0:
+                nc.vector.tensor_copy(dst[:, :v_cols], src[:, :v_cols])
+            if v_cols < P:
+                nc.scalar.copy(dst[:, v_cols:], src[:, v_cols:])
+            return grouped
+
+        def quantize(name, o, grouped):
+            codes[name, o] = keep.tile([P, H], U32, name="codes_%s%d" % (name, o), align_bytes=64)
+            planes[name, o] = keep.tile([P, H], U8, name="plane_%s%d" % (name, o), align_bytes=64)
+            nc.vector.quantize_mx(codes[name, o][:].bitcast(FP8X4), planes[name, o][:], grouped[:])
+
+        nc.vector.tensor_copy(dealt(xs), x_planes[:].indirect(offs_sb[:]))
+        nc.vector.tensor_copy(dealt(xw[0]), x_table[0][:].indirect(offs_sb[:]))
+        quantize("w2", 0, interleave("w2", 0, 64))
+        nc.vector.tensor_copy(dealt(xw[1]), x_table[1][:].indirect(offs_sb[:]))
+        quantize("w2", 1, interleave("w2", 1, 80))
+
+        def product(bank_cols, name, jt, cols):
+            jcols = slice(jt * P, (jt + 1) * P)
+            for o in range(PASSES):
+                nc.tensor.matmul_mx(
+                    out=bank_cols,
+                    lhsT=xw[o][:, jcols].bitcast(FP8X4),
+                    lhsT_scale=xs[4 * o : P, jcols],
+                    rhs=codes[name, o][:, cols].bitcast(FP8X4),
+                    rhs_scale=planes[name, o][:, cols],
+                    start=(o == 0),
+                    stop=(o == PASSES - 1),
+                )
+
+        def sum_over_d(bank_cols, sources):
+            for d, src in enumerate(sources):
+                nc.tensor.matmul(bank_cols, src, ident[:], start=(d == 0), stop=(d == D - 1), is_transpose=True)
+
+        visi = [keep.tile([P, D, H], F32, name="visi%d" % h) for h in range(2)]
+        open_acc = [acc.tile([P, 2, V], F32, name="acc") for th in range(2)]
+        for h in range(2):
+            for d in range(D):
+                bank = mm.tile([P, H], F32, name="bank")
+                product(bank[:], "w2", h * D + d, slice(0, H))
+                nc.scalar.activation(visi[h][:, d, :], bank[:], ACT.Sigmoid, scale=2.0)
+            for t in range(PACK):
+                sum_over_d(
+                    open_acc[t // 2][:, t % 2, h * P : (h + 1) * P],
+                    [visi[h][:, d, t * P : (t + 1) * P] for d in range(D)],
+                )
+
+        quantize("w1", 0, interleave("w1", 0, P))
+        quantize("w1", 1, interleave("w1", 1, P))
+
+        shade = keep.tile([P, PACK, U], F32, name="shade")
+        for t in range(PACK):
+            nc.scalar.activation(closed[t][:, :V], open_acc[t // 2][:, t % 2, :], ACT.Copy, bias=0.8, scale=-0.8 / D)
+            nc.scalar.activation(shade[:, t, :], closed[t][:].indirect(va_sb[:]), ACT.Copy)
+
+        grouped3 = keep.tile([P, N * PACK], BF16, name="grouped3", align_bytes=64)
+        codes3 = keep.tile([P, N], U32, name="codes3", align_bytes=64)
+        plane3 = keep.tile([P, N], U8, name="plane3", align_bytes=64)
+
+        own = keep.tile([P, PACK, U], F32, name="own")
+        other = keep.tile([P, PACK, U], F32, name="other")
+
+        def fetch(t, r0, r1):
+            lst = slice(r0 // 16, r1 // 16)
+            nc.vector.tensor_tensor(other[:, t, r0:r1], direct[t][:].indirect(vb_sb[:, lst]), shade[:, t, r0:r1], ALU.mult)
+            nc.scalar.activation(own[:, t, r0:r1], direct[t][:].indirect(va_sb[:, lst]), ACT.Copy)
+
+        for th in range(2):
+            cols = slice(th * 2 * P, (th + 1) * 2 * P)
+            direct_acc = acc.tile([P, 2, V], F32, name="acc")
+            for h in range(2):
+                lit = keep.tile([P, D, 2 * P], F32, name="lit%d%d" % (th, h))
+                for dd in range(2):
+                    bank = mm.tile([P, 2, 2 * P], F32, name="bank")
+                    for dl in range(2):
+                        product(bank[:, dl, :], "w1", h * D + 2 * dd + dl, cols)
+                    nc.vector.tensor_tensor(
+                        lit[:, 2 * dd : 2 * dd + 2, :], bank[:], visi[h][:, 2 * dd : 2 * dd + 2, cols], ALU.mult
+                    )
+                for tl in range(2):
+                    sum_over_d(
+                        direct_acc[:, tl, h * P : (h + 1) * P],
+                        [lit[:, d, tl * P : (tl + 1) * P] for d in range(D)],
+                    )
+            for tl in range(2):
+                t = 2 * th + tl
+                nc.scalar.activation(direct[t][:, :V], direct_acc[:, tl, :], ACT.Copy, scale=unit_sb[:, t : t + 1])
+            if th == 0:
+                nc.vector.tensor_copy(
+                    grouped3[:].rearrange("p (c i j) -> p c j i", i=4, j=PACK),
+                    raw3[:].rearrange("p j (c i) -> p c j i", i=4),
+                )
+                nc.vector.quantize_mx(codes3[:].bitcast(FP8X4), plane3[:], grouped3[:])
+                for tl in range(2):
+                    fetch(tl, 0, U)
+
+        R = U // 2
+        for rh in range(2):
+            r0, r1 = rh * R, (rh + 1) * R
+            for t in (2, 3):
+                fetch(t, r0, r1)
+            hid = keep.tile([P, R * PACK], BF16, name="hid%d" % rh, align_bytes=64)
+            nc.vector.tensor_tensor(
+                hid[:].rearrange("p (c i t) -> p c t i", i=4, t=PACK),
+                own[:, :, r0:r1].rearrange("p t (c i) -> p c t i", i=4),
+                other[:, :, r0:r1].rearrange("p t (c i) -> p c t i", i=4),
+                ALU.add,
+            )
+            hid_codes = keep.tile([P, R], U32, name="hid_codes%d" % rh, align_bytes=64)
+            hid_plane = keep.tile([P, R], U8, name="hid_plane%d" % rh, align_bytes=64)
+            nc.vector.quantize_mx(hid_codes[:].bitcast(FP8X4), hid_plane[:], hid[:])
+            bank = mm.tile([P, 2, R], F32, name="bank")
+            for mt in range(2):
+                nc.tensor.matmul_mx(
+                    out=bank[:, mt, :],
+                    lhsT=codes3[:, mt * P : (mt + 1) * P].bitcast(FP8X4),
+                    lhsT_scale=plane3[:, mt * P : (mt + 1) * P],
+                    rhs=hid_codes[:].bitcast(FP8X4),
+                    rhs_scale=hid_plane[:],
+                    start=True,
+                    stop=True,
+                )
+            result = keep.tile([P, 2, R], F32, name="result%d" % rh)
+            nc.scalar.copy(result[:], bank[:])
+            nc.sync.dma_start(out[:, r0:r1].rearrange("(mt p) r -> p mt r", p=P), result[:])

@@ -20,7 +20,11 @@ P = 128
 PACK = 4
 K_PASS = P * PACK
 PASSES = K // K_PASS
-WINDOW = U + 16
+LIST_ROWS = 16
+WINDOW = U + LIST_ROWS
+HALF = H // 2
+POINTS = U // 2
+SCALAR_ROWS = 96
 
 
 def tile_picked_yprtrn_lin_p_kernel(
@@ -29,22 +33,17 @@ def tile_picked_yprtrn_lin_p_kernel(
     nc = tc.nc
     with ExitStack() as ctx:
         keep = ctx.enter_context(tc.tile_pool(name="keep", bufs=1))
-        mm = ctx.enter_context(tc.psum_pool(name="mm", bufs=6))
-        acc = ctx.enter_context(tc.psum_pool(name="acc", bufs=2))
+        psum = ctx.enter_context(tc.psum_pool(name="psum", bufs=1))
 
-        offs_sb = keep.tile([P, S // 16], U16, name="offs_sb")
-        va_sb = keep.tile([P, U // 16], U16, name="va_sb")
-        vb_sb = keep.tile([P, U // 16], U16, name="vb_sb")
+        offs_sb = keep.tile([P, S // LIST_ROWS], U16, name="offs_sb")
+        va_sb = keep.tile([P, U // LIST_ROWS], U16, name="va_sb")
+        vb_sb = keep.tile([P, U // LIST_ROWS], U16, name="vb_sb")
         x_planes = keep.tile([P, T], U8, name="x_planes")
         nc.gpsimd.memset(x_planes[:].bitcast(I32), 0)
         nc.sync.dma_start(offs_sb[:], offs)
 
         x_table = [keep.tile([P, T], U32, name="x_table%d" % o) for o in range(PASSES)]
-        raw = {
-            (name, o): keep.tile([P, PACK, H], F32, name="raw_%s%d" % (name, o))
-            for name in ("w2", "w1")
-            for o in range(PASSES)
-        }
+        raw = {}
         raw3 = keep.tile([P, PACK, N], F32, name="raw3")
         unit_sb = keep.tile([P, PACK], F32, name="unit_sb")
 
@@ -54,21 +53,23 @@ def tile_picked_yprtrn_lin_p_kernel(
                 x_words[o].rearrange("p n t -> p (n t)").bitcast(I32),
             )
 
-        def load_w(name, w, o):
-            rows = w[o * K_PASS : (o + 1) * K_PASS, :]
-            nc.sync.dma_start(raw[name, o][:], rows.rearrange("(p j) c -> p j c", j=PACK))
+        def load_w(name, w, o, c0, c1):
+            rows = w[o * K_PASS : (o + 1) * K_PASS, c0:c1]
+            raw[name, o, c0] = keep.tile([P, PACK, c1 - c0], F32, name="raw_%s%d_%d" % (name, o, c0))
+            nc.sync.dma_start(raw[name, o, c0][:], rows.rearrange("(p j) c -> p j c", j=PACK))
 
+        load_x(0)
         for q in range(4):
             nc.sync.dma_start(
-                x_planes[32 * q : 32 * q + 8, :].bitcast(I32),
+                x_planes[32 * q : 32 * q + 4 * PASSES, :].bitcast(I32),
                 x_scales[:, 4 * q : 4 * q + 4, :].bitcast(I32),
             )
-        load_x(0)
-        load_w("w2", w2, 0)
+        load_w("w2", w2, 0, 0, H)
         load_x(1)
-        load_w("w2", w2, 1)
-        load_w("w1", w1, 0)
-        load_w("w1", w1, 1)
+        load_w("w2", w2, 1, 0, H)
+        load_w("w1", w1, 0, 0, H)
+        load_w("w1", w1, 1, 0, H // 2)
+        load_w("w1", w1, 1, H // 2, H)
         nc.sync.dma_start(va_sb[:], va)
         nc.sync.dma_start(vb_sb[:], vb2)
         nc.sync.dma_start(unit_sb[:], unit.rearrange("(p t) o -> p (t o)", t=PACK))
@@ -77,138 +78,167 @@ def tile_picked_yprtrn_lin_p_kernel(
         ident = keep.tile([P, P], F32, name="ident")
         make_identity(nc, ident[:])
 
+        half_unit = keep.tile([P, PACK], F32, name="half_unit")
+        nc.vector.tensor_scalar(half_unit[:], unit_sb[:], 0.5, 0.0, ALU.mult, ALU.add)
+
         closed = [keep.tile([P, WINDOW], F32, name="closed%d" % t) for t in range(PACK)]
         direct = [keep.tile([P, WINDOW], F32, name="direct%d" % t) for t in range(PACK)]
         for table in closed + direct:
-            nc.gpsimd.memset(table[:, V:], 0.0)
+            nc.vector.memset(table[:, V:], 0.0)
 
-        def dealt(tile):
-            return tile[:].rearrange("p (h d v) -> p h v d", h=2, d=D)
+        def dealt(ap):
+            return ap.rearrange("p (h d v) -> p h v d", d=D, v=P)
 
         xs = keep.tile([P, S], U8, name="xs", align_bytes=64)
-        xw = [keep.tile([P, S], U32, name="xw%d" % o, align_bytes=64) for o in range(PASSES)]
 
         codes, planes = {}, {}
 
-        def interleave(name, o, v_cols):
-            grouped = keep.tile([P, PACK * H], BF16, name="grp_%s%d" % (name, o), align_bytes=64)
+        def interleave(name, o, shares, tag):
+            grouped = keep.tile([P, PACK * H], BF16, name="grp_%s%d" % (name, o), tag=tag, align_bytes=64)
             dst = grouped[:].rearrange("p (t m j) -> p m j t", t=PACK, j=PACK)
-            src = raw[name, o][:].rearrange("p j (m t) -> p m j t", t=PACK)
-            if v_cols > 0:
-                nc.vector.tensor_copy(dst[:, :v_cols], src[:, :v_cols])
-            if v_cols < P:
-                nc.scalar.copy(dst[:, v_cols:], src[:, v_cols:])
+            for copy, c0, m0, m1, t0, t1 in shares:
+                src = raw[name, o, c0][:].rearrange("p j (m t) -> p m j t", t=PACK)
+                copy(dst[:, m0:m1, :, t0:t1], src[:, m0 - c0 // PACK : m1 - c0 // PACK, :, t0:t1])
             return grouped
 
-        def quantize(name, o, grouped):
+        def quantize(name, o, grouped, parts):
             codes[name, o] = keep.tile([P, H], U32, name="codes_%s%d" % (name, o), align_bytes=64)
             planes[name, o] = keep.tile([P, H], U8, name="plane_%s%d" % (name, o), align_bytes=64)
-            nc.vector.quantize_mx(codes[name, o][:].bitcast(FP8X4), planes[name, o][:], grouped[:])
-
-        nc.vector.tensor_copy(dealt(xs), x_planes[:].indirect(offs_sb[:]))
-        nc.vector.tensor_copy(dealt(xw[0]), x_table[0][:].indirect(offs_sb[:]))
-        quantize("w2", 0, interleave("w2", 0, 64))
-        nc.vector.tensor_copy(dealt(xw[1]), x_table[1][:].indirect(offs_sb[:]))
-        quantize("w2", 1, interleave("w2", 1, 80))
-
-        def product(bank_cols, name, jt, cols):
-            jcols = slice(jt * P, (jt + 1) * P)
-            for o in range(PASSES):
-                nc.tensor.matmul_mx(
-                    out=bank_cols,
-                    lhsT=xw[o][:, jcols].bitcast(FP8X4),
-                    lhsT_scale=xs[4 * o : P, jcols],
-                    rhs=codes[name, o][:, cols].bitcast(FP8X4),
-                    rhs_scale=planes[name, o][:, cols],
-                    start=(o == 0),
-                    stop=(o == PASSES - 1),
+            for lo, hi in parts:
+                nc.vector.quantize_mx(
+                    codes[name, o][:, lo:hi].bitcast(FP8X4), planes[name, o][:, lo:hi], grouped[:, PACK * lo : PACK * hi]
                 )
 
-        def sum_over_d(bank_cols, sources):
-            for d, src in enumerate(sources):
-                nc.tensor.matmul(bank_cols, src, ident[:], start=(d == 0), stop=(d == D - 1), is_transpose=True)
+        on_v, on_s = nc.vector.tensor_copy, nc.scalar.copy
+        whole, halves = ((0, H),), ((0, HALF), (HALF, H))
+        xw0 = keep.tile([P, S], U32, name="xw0", align_bytes=64)
+        nc.vector.tensor_copy(dealt(xw0[:]), x_table[0][:].indirect(offs_sb[:]))
+        nc.vector.tensor_copy(dealt(xs[:]), x_planes[:].indirect(offs_sb[:]))
+        quantize("w2", 0, interleave("w2", 0, [(on_s, 0, 0, P, 0, PACK)], "first"), whole)
+        xw1 = keep.tile([P, S], U32, name="xw1", tag="first", align_bytes=64)
+        nc.vector.tensor_copy(dealt(xw1[:]), x_table[1][:].indirect(offs_sb[:]))
+        xw = [xw0, xw1]
+        shares = [(on_s, 0, 0, P, 0, 2), (on_s, 0, 0, SCALAR_ROWS, 2, PACK), (on_v, 0, SCALAR_ROWS, P, 2, PACK)]
+        quantize("w2", 1, interleave("w2", 1, shares, "second"), halves)
 
-        visi = [keep.tile([P, D, H], F32, name="visi%d" % h) for h in range(2)]
-        open_acc = [acc.tile([P, 2, V], F32, name="acc") for th in range(2)]
-        for h in range(2):
+        def product(name, h, dd, th, b, order):
+            bank = psum.tile([P, 2, HALF], F32, name="bank%d" % b)
+            cols = slice(th * HALF, (th + 1) * HALF)
+            for o in order:
+                for dl in range(2):
+                    jt = h * D + 2 * dd + dl
+                    jcols = slice(jt * P, (jt + 1) * P)
+                    nc.tensor.matmul_mx(
+                        out=bank[:, dl, :],
+                        lhsT=xw[o][:, jcols].bitcast(FP8X4),
+                        lhsT_scale=xs[4 * o : P, jcols],
+                        rhs=codes[name, o][:, cols].bitcast(FP8X4),
+                        rhs_scale=planes[name, o][:, cols],
+                        start=(o == order[0] and dl == 0),
+                        stop=(o == order[-1] and dl == 1),
+                    )
+            return bank
+
+        def sum_over_d(total, terms, tl):
             for d in range(D):
-                bank = mm.tile([P, H], F32, name="bank")
-                product(bank[:], "w2", h * D + d, slice(0, H))
-                nc.scalar.activation(visi[h][:, d, :], bank[:], ACT.Sigmoid, scale=2.0)
-            for t in range(PACK):
-                sum_over_d(
-                    open_acc[t // 2][:, t % 2, h * P : (h + 1) * P],
-                    [visi[h][:, d, t * P : (t + 1) * P] for d in range(D)],
+                nc.tensor.matmul(
+                    total, terms[:, d, tl * P : (tl + 1) * P], ident[:], start=(d == 0), stop=(d == D - 1), is_transpose=True
                 )
 
-        quantize("w1", 0, interleave("w1", 0, P))
-        quantize("w1", 1, interleave("w1", 1, P))
+        tanh_yv = {}
+        for th in range(2):
+            for h in range(2):
+                tag = "tanh%d%d" % (th, h)
+                tanh_yv[th, h] = keep.tile([P, D, HALF], F32, name=tag, tag=tag, align_bytes=64)
+        for th in range(2):
+            for h in range(2):
+                for dd in range(2):
+                    bank = product("w2", h, dd, th, 4 * th + 2 * h + dd, (0, 1))
+                    nc.scalar.activation(tanh_yv[th, h][:, 2 * dd : 2 * dd + 2, :], bank[:], ACT.Tanh)
+
+        tanh_sum = []
+        for th in range(2):
+            tanh_sum.append(psum.tile([P, 2, V], F32, name="bank%d" % (4 * th)))
+            for h in range(2):
+                for tl in range(2):
+                    sum_over_d(tanh_sum[th][:, tl, h * P : (h + 1) * P], tanh_yv[th, h], tl)
 
         shade = keep.tile([P, PACK, U], F32, name="shade")
+        other = keep.tile([P, PACK, U], F32, name="other")
         for t in range(PACK):
-            nc.scalar.activation(closed[t][:, :V], open_acc[t // 2][:, t % 2, :], ACT.Copy, bias=0.8, scale=-0.8 / D)
+            nc.scalar.activation(closed[t][:, :V], tanh_sum[t // 2][:, t % 2, :], ACT.Copy, bias=0.4, scale=-0.4 / D)
             nc.scalar.activation(shade[:, t, :], closed[t][:].indirect(va_sb[:]), ACT.Copy)
 
-        grouped3 = keep.tile([P, N * PACK], BF16, name="grouped3", align_bytes=64)
-        codes3 = keep.tile([P, N], U32, name="codes3", align_bytes=64)
-        plane3 = keep.tile([P, N], U8, name="plane3", align_bytes=64)
+        quantize("w1", 0, interleave("w1", 0, [(on_v, 0, 0, P, 0, PACK)], "second"), whole)
+        shares = [(on_v, 0, 0, P // 2, 0, PACK), (on_v, H // 2, P // 2, P, 0, PACK)]
+        quantize("w1", 1, interleave("w1", 1, shares, "third"), halves)
 
-        own = keep.tile([P, PACK, U], F32, name="own")
-        other = keep.tile([P, PACK, U], F32, name="other")
-
-        def fetch(t, r0, r1):
-            lst = slice(r0 // 16, r1 // 16)
-            nc.vector.tensor_tensor(other[:, t, r0:r1], direct[t][:].indirect(vb_sb[:, lst]), shade[:, t, r0:r1], ALU.mult)
-            nc.scalar.activation(own[:, t, r0:r1], direct[t][:].indirect(va_sb[:, lst]), ACT.Copy)
-
+        lit = {}
+        y_banks = (1, 2, 3, 5, 6, 7)
         for th in range(2):
-            cols = slice(th * 2 * P, (th + 1) * 2 * P)
-            direct_acc = acc.tile([P, 2, V], F32, name="acc")
             for h in range(2):
-                lit = keep.tile([P, D, 2 * P], F32, name="lit%d%d" % (th, h))
+                lit[th, h] = keep.tile([P, D, HALF], F32, name="lit%d%d" % (th, h), tag="lit%d%d" % (th, h))
                 for dd in range(2):
-                    bank = mm.tile([P, 2, 2 * P], F32, name="bank")
-                    for dl in range(2):
-                        product(bank[:, dl, :], "w1", h * D + 2 * dd + dl, cols)
-                    nc.vector.tensor_tensor(
-                        lit[:, 2 * dd : 2 * dd + 2, :], bank[:], visi[h][:, 2 * dd : 2 * dd + 2, cols], ALU.mult
+                    turn = 4 * th + 2 * h + dd
+                    bank = product("w1", h, dd, th, y_banks[turn % len(y_banks)], (0, 1) if turn == 0 else (1, 0))
+                    nc.vector.scalar_tensor_tensor(
+                        lit[th, h][:, 2 * dd : 2 * dd + 2, :],
+                        tanh_yv[th, h][:, 2 * dd : 2 * dd + 2, :],
+                        1.0,
+                        bank[:],
+                        ALU.add,
+                        ALU.mult,
                     )
-                for tl in range(2):
-                    sum_over_d(
-                        direct_acc[:, tl, h * P : (h + 1) * P],
-                        [lit[:, d, tl * P : (tl + 1) * P] for d in range(D)],
-                    )
-            for tl in range(2):
-                t = 2 * th + tl
-                nc.scalar.activation(direct[t][:, :V], direct_acc[:, tl, :], ACT.Copy, scale=unit_sb[:, t : t + 1])
-            if th == 0:
-                nc.vector.tensor_copy(
-                    grouped3[:].rearrange("p (c i j) -> p c j i", i=4, j=PACK),
-                    raw3[:].rearrange("p j (c i) -> p c j i", i=4),
-                )
-                nc.vector.quantize_mx(codes3[:].bitcast(FP8X4), plane3[:], grouped3[:])
-                for tl in range(2):
-                    fetch(tl, 0, U)
 
-        R = U // 2
+        grouped3 = keep.tile([P, N * PACK], BF16, name="grouped3", tag="third", align_bytes=64)
+        codes3 = keep.tile([P, N], U32, name="codes3", tag="tanh11", align_bytes=64)
+        plane3 = keep.tile([P, N], U8, name="plane3", align_bytes=64)
+        nc.gpsimd.tensor_scalar(
+            grouped3[:].rearrange("p (c j) -> p c j", j=PACK),
+            raw3[:].rearrange("p j c -> p c j"),
+            1.0,
+            0.0,
+            ALU.mult,
+            ALU.add,
+        )
+        nc.vector.quantize_mx(codes3[:].bitcast(FP8X4), plane3[:], grouped3[:])
+
+        for t, b in enumerate(y_banks[2:]):
+            th, tl = divmod(t, 2)
+            total = psum.tile([P, V], F32, name="bank%d" % b)
+            for h in range(2):
+                sum_over_d(total[:, h * P : (h + 1) * P], lit[th, h], tl)
+            if t == 0:
+                nc.vector.tensor_scalar(direct[t][:, :V], total[:], half_unit[:, t : t + 1], None, ALU.mult)
+            else:
+                nc.scalar.activation(direct[t][:, :V], total[:], ACT.Copy, scale=half_unit[:, t : t + 1])
+
+        for t in range(PACK):
+            nc.vector.tensor_tensor(other[:, t, :], direct[t][:].indirect(vb_sb[:]), shade[:, t, :], ALU.mult)
+
+        own = keep.tile([P, PACK, U], F32, name="own", tag="lit11")
+        out_banks = ((0, 4), (1, 2))
         for rh in range(2):
-            r0, r1 = rh * R, (rh + 1) * R
-            for t in (2, 3):
-                fetch(t, r0, r1)
-            hid = keep.tile([P, R * PACK], BF16, name="hid%d" % rh, align_bytes=64)
+            r0, r1 = rh * POINTS, (rh + 1) * POINTS
+            for t in range(PACK):
+                nc.scalar.activation(
+                    own[:, t, r0:r1], direct[t][:].indirect(va_sb[:, r0 // LIST_ROWS : r1 // LIST_ROWS]), ACT.Copy
+                )
+            hid = keep.tile([P, POINTS * PACK], BF16, name="hid%d" % rh, align_bytes=64)
             nc.vector.tensor_tensor(
                 hid[:].rearrange("p (c i t) -> p c t i", i=4, t=PACK),
                 own[:, :, r0:r1].rearrange("p t (c i) -> p c t i", i=4),
                 other[:, :, r0:r1].rearrange("p t (c i) -> p c t i", i=4),
                 ALU.add,
             )
-            hid_codes = keep.tile([P, R], U32, name="hid_codes%d" % rh, align_bytes=64)
-            hid_plane = keep.tile([P, R], U8, name="hid_plane%d" % rh, align_bytes=64)
+            hid_codes = keep.tile([P, POINTS], U32, name="hid_codes%d" % rh, align_bytes=64)
+            hid_plane = keep.tile([P, POINTS], U8, name="hid_plane%d" % rh, align_bytes=64)
             nc.vector.quantize_mx(hid_codes[:].bitcast(FP8X4), hid_plane[:], hid[:])
-            bank = mm.tile([P, 2, R], F32, name="bank")
-            for mt in range(2):
+            result = keep.tile([P, N // P, POINTS], F32, name="result%d" % rh)
+            for mt in range(N // P):
+                bank = psum.tile([P, POINTS], F32, name="bank%d" % out_banks[rh][mt])
                 nc.tensor.matmul_mx(
-                    out=bank[:, mt, :],
+                    out=bank[:],
                     lhsT=codes3[:, mt * P : (mt + 1) * P].bitcast(FP8X4),
                     lhsT_scale=plane3[:, mt * P : (mt + 1) * P],
                     rhs=hid_codes[:].bitcast(FP8X4),
@@ -216,6 +246,6 @@ def tile_picked_yprtrn_lin_p_kernel(
                     start=True,
                     stop=True,
                 )
-            result = keep.tile([P, 2, R], F32, name="result%d" % rh)
-            nc.scalar.copy(result[:], bank[:])
+                leave = on_v if (rh, mt) == (1, 1) else on_s
+                leave(result[:, mt, :], bank[:])
             nc.sync.dma_start(out[:, r0:r1].rearrange("(mt p) r -> p mt r", p=P), result[:])

from contextlib import ExitStack

import concourse.mybir as mybir
from concourse.masks import make_identity

K, T, S, D, N, H, V, U = 1024, 2048, 1024, 4, 256, 512, 256, 512
FLOPS = 2 * (2 * K * H * S + H * N * U)

F32 = mybir.dt.float32
BF16 = mybir.dt.bfloat16
I32 = mybir.dt.int32
U32 = mybir.dt.uint32
U16 = mybir.dt.uint16
U8 = mybir.dt.uint8
FP8X4 = mybir.dt.float8_e4m3fn_x4
ACT = mybir.ActivationFunctionType
ALU = mybir.AluOpType

P = 128
PACK = 4
K_PASS = P * PACK
PASSES = K // K_PASS
LIST_ROWS = 16
WINDOW = U + LIST_ROWS
HALF = H // 2
POINTS = U // 2
SCALAR_ROWS = 96


def tile_picked_yprtrn_lin_p_kernel(
    tc, x_words, x_scales, w1, w2, unit, w3, offs, va, vb2, out
):
    nc = tc.nc
    with ExitStack() as ctx:
        keep = ctx.enter_context(tc.tile_pool(name="keep", bufs=1))
        psum = ctx.enter_context(tc.psum_pool(name="psum", bufs=1))

        offs_sb = keep.tile([P, S // LIST_ROWS], U16, name="offs_sb")
        va_sb = keep.tile([P, U // LIST_ROWS], U16, name="va_sb")
        vb_sb = keep.tile([P, U // LIST_ROWS], U16, name="vb_sb")
        x_planes = keep.tile([P, T], U8, name="x_planes")
        nc.gpsimd.memset(x_planes[:].bitcast(I32), 0)
        nc.sync.dma_start(offs_sb[:], offs)

        x_table = [keep.tile([P, T], U32, name="x_table%d" % o) for o in range(PASSES)]
        raw = {}
        raw3 = keep.tile([P, PACK, N], F32, name="raw3")
        unit_sb = keep.tile([P, PACK], F32, name="unit_sb")

        def load_x(o):
            nc.sync.dma_start(
                x_table[o][:].bitcast(I32),
                x_words[o].rearrange("p n t -> p (n t)").bitcast(I32),
            )

        def load_w(name, w, o, c0, c1):
            rows = w[o * K_PASS : (o + 1) * K_PASS, c0:c1]
            raw[name, o, c0] = keep.tile([P, PACK, c1 - c0], F32, name="raw_%s%d_%d" % (name, o, c0))
            nc.sync.dma_start(raw[name, o, c0][:], rows.rearrange("(p j) c -> p j c", j=PACK))

        load_x(0)
        for q in range(4):
            nc.sync.dma_start(
                x_planes[32 * q : 32 * q + 4 * PASSES, :].bitcast(I32),
                x_scales[:, 4 * q : 4 * q + 4, :].bitcast(I32),
            )
        load_w("w2", w2, 0, 0, H)
        load_x(1)
        load_w("w2", w2, 1, 0, H)
        load_w("w1", w1, 0, 0, H)
        load_w("w1", w1, 1, 0, H // 2)
        load_w("w1", w1, 1, H // 2, H)
        nc.sync.dma_start(va_sb[:], va)
        nc.sync.dma_start(vb_sb[:], vb2)
        nc.sync.dma_start(unit_sb[:], unit.rearrange("(p t) o -> p (t o)", t=PACK))
        nc.sync.dma_start(raw3[:], w3.rearrange("(p j) c -> p j c", j=PACK))

        ident = keep.tile([P, P], F32, name="ident")
        make_identity(nc, ident[:])

        half_unit = keep.tile([P, PACK], F32, name="half_unit")
        nc.vector.tensor_scalar(half_unit[:], unit_sb[:], 0.5, 0.0, ALU.mult, ALU.add)

        closed = [keep.tile([P, WINDOW], F32, name="closed%d" % t) for t in range(PACK)]
        direct = [keep.tile([P, WINDOW], F32, name="direct%d" % t) for t in range(PACK)]
        for table in closed + direct:
            nc.vector.memset(table[:, V:], 0.0)

        def dealt(ap):
            return ap.rearrange("p (h d v) -> p h v d", d=D, v=P)

        xs = keep.tile([P, S], U8, name="xs", align_bytes=64)

        codes, planes = {}, {}

        def interleave(name, o, shares, tag):
            grouped = keep.tile([P, PACK * H], BF16, name="grp_%s%d" % (name, o), tag=tag, align_bytes=64)
            dst = grouped[:].rearrange("p (t m j) -> p m j t", t=PACK, j=PACK)
            for copy, c0, m0, m1, t0, t1 in shares:
                src = raw[name, o, c0][:].rearrange("p j (m t) -> p m j t", t=PACK)
                copy(dst[:, m0:m1, :, t0:t1], src[:, m0 - c0 // PACK : m1 - c0 // PACK, :, t0:t1])
            return grouped

        def quantize(name, o, grouped, parts):
            codes[name, o] = keep.tile([P, H], U32, name="codes_%s%d" % (name, o), align_bytes=64)
            planes[name, o] = keep.tile([P, H], U8, name="plane_%s%d" % (name, o), align_bytes=64)
            for lo, hi in parts:
                nc.vector.quantize_mx(
                    codes[name, o][:, lo:hi].bitcast(FP8X4), planes[name, o][:, lo:hi], grouped[:, PACK * lo : PACK * hi]
                )

        on_v, on_s = nc.vector.tensor_copy, nc.scalar.copy
        whole, halves = ((0, H),), ((0, HALF), (HALF, H))
        xw0 = keep.tile([P, S], U32, name="xw0", align_bytes=64)
        nc.vector.tensor_copy(dealt(xw0[:]), x_table[0][:].indirect(offs_sb[:]))
        nc.vector.tensor_copy(dealt(xs[:]), x_planes[:].indirect(offs_sb[:]))
        quantize("w2", 0, interleave("w2", 0, [(on_s, 0, 0, P, 0, PACK)], "first"), whole)
        xw1 = keep.tile([P, S], U32, name="xw1", tag="first", align_bytes=64)
        nc.vector.tensor_copy(dealt(xw1[:]), x_table[1][:].indirect(offs_sb[:]))
        xw = [xw0, xw1]
        shares = [(on_s, 0, 0, P, 0, 2), (on_s, 0, 0, SCALAR_ROWS, 2, PACK), (on_v, 0, SCALAR_ROWS, P, 2, PACK)]
        quantize("w2", 1, interleave("w2", 1, shares, "second"), halves)

        def product(name, h, dd, th, b, order):
            bank = psum.tile([P, 2, HALF], F32, name="bank%d" % b)
            cols = slice(th * HALF, (th + 1) * HALF)
            for o in order:
                for dl in range(2):
                    jt = h * D + 2 * dd + dl
                    jcols = slice(jt * P, (jt + 1) * P)
                    nc.tensor.matmul_mx(
                        out=bank[:, dl, :],
                        lhsT=xw[o][:, jcols].bitcast(FP8X4),
                        lhsT_scale=xs[4 * o : P, jcols],
                        rhs=codes[name, o][:, cols].bitcast(FP8X4),
                        rhs_scale=planes[name, o][:, cols],
                        start=(o == order[0] and dl == 0),
                        stop=(o == order[-1] and dl == 1),
                    )
            return bank

        def sum_over_d(total, terms, tl):
            for d in range(D):
                nc.tensor.matmul(
                    total, terms[:, d, tl * P : (tl + 1) * P], ident[:], start=(d == 0), stop=(d == D - 1), is_transpose=True
                )

        tanh_yv = {}
        for th in range(2):
            for h in range(2):
                tag = "tanh%d%d" % (th, h)
                tanh_yv[th, h] = keep.tile([P, D, HALF], F32, name=tag, tag=tag, align_bytes=64)
        for th in range(2):
            for h in range(2):
                for dd in range(2):
                    bank = product("w2", h, dd, th, 4 * th + 2 * h + dd, (0, 1))
                    nc.scalar.activation(tanh_yv[th, h][:, 2 * dd : 2 * dd + 2, :], bank[:], ACT.Tanh)

        tanh_sum = []
        for th in range(2):
            tanh_sum.append(psum.tile([P, 2, V], F32, name="bank%d" % (4 * th)))
            for h in range(2):
                for tl in range(2):
                    sum_over_d(tanh_sum[th][:, tl, h * P : (h + 1) * P], tanh_yv[th, h], tl)

        shade = keep.tile([P, PACK, U], F32, name="shade")
        other = keep.tile([P, PACK, U], F32, name="other")
        for t in range(PACK):
            nc.scalar.activation(closed[t][:, :V], tanh_sum[t // 2][:, t % 2, :], ACT.Copy, bias=0.4, scale=-0.4 / D)
            nc.scalar.activation(shade[:, t, :], closed[t][:].indirect(va_sb[:]), ACT.Copy)

        quantize("w1", 0, interleave("w1", 0, [(on_v, 0, 0, P, 0, PACK)], "second"), whole)
        shares = [(on_v, 0, 0, P // 2, 0, PACK), (on_v, H // 2, P // 2, P, 0, PACK)]
        quantize("w1", 1, interleave("w1", 1, shares, "third"), halves)

        lit = {}
        y_banks = (1, 2, 3, 5, 6, 7)
        for th in range(2):
            for h in range(2):
                lit[th, h] = keep.tile([P, D, HALF], F32, name="lit%d%d" % (th, h), tag="lit%d%d" % (th, h))
                for dd in range(2):
                    turn = 4 * th + 2 * h + dd
                    bank = product("w1", h, dd, th, y_banks[turn % len(y_banks)], (0, 1) if turn == 0 else (1, 0))
                    nc.vector.scalar_tensor_tensor(
                        lit[th, h][:, 2 * dd : 2 * dd + 2, :],
                        tanh_yv[th, h][:, 2 * dd : 2 * dd + 2, :],
                        1.0,
                        bank[:],
                        ALU.add,
                        ALU.mult,
                    )

        grouped3 = keep.tile([P, N * PACK], BF16, name="grouped3", tag="third", align_bytes=64)
        codes3 = keep.tile([P, N], U32, name="codes3", tag="tanh11", align_bytes=64)
        plane3 = keep.tile([P, N], U8, name="plane3", align_bytes=64)
        nc.gpsimd.tensor_scalar(
            grouped3[:].rearrange("p (c j) -> p c j", j=PACK),
            raw3[:].rearrange("p j c -> p c j"),
            1.0,
            0.0,
            ALU.mult,
            ALU.add,
        )
        nc.vector.quantize_mx(codes3[:].bitcast(FP8X4), plane3[:], grouped3[:])

        for t, b in enumerate(y_banks[2:]):
            th, tl = divmod(t, 2)
            total = psum.tile([P, V], F32, name="bank%d" % b)
            for h in range(2):
                sum_over_d(total[:, h * P : (h + 1) * P], lit[th, h], tl)
            if t == 0:
                nc.vector.tensor_scalar(direct[t][:, :V], total[:], half_unit[:, t : t + 1], None, ALU.mult)
            else:
                nc.scalar.activation(direct[t][:, :V], total[:], ACT.Copy, scale=half_unit[:, t : t + 1])

        for t in range(PACK):
            nc.vector.tensor_tensor(other[:, t, :], direct[t][:].indirect(vb_sb[:]), shade[:, t, :], ALU.mult)

        own = keep.tile([P, PACK, U], F32, name="own", tag="lit11")
        out_banks = ((0, 4), (1, 2))
        for rh in range(2):
            r0, r1 = rh * POINTS, (rh + 1) * POINTS
            for t in range(PACK):
                nc.scalar.activation(
                    own[:, t, r0:r1], direct[t][:].indirect(va_sb[:, r0 // LIST_ROWS : r1 // LIST_ROWS]), ACT.Copy
                )
            hid = keep.tile([P, POINTS * PACK], BF16, name="hid%d" % rh, align_bytes=64)
            nc.vector.tensor_tensor(
                hid[:].rearrange("p (c i t) -> p c t i", i=4, t=PACK),
                own[:, :, r0:r1].rearrange("p t (c i) -> p c t i", i=4),
                other[:, :, r0:r1].rearrange("p t (c i) -> p c t i", i=4),
                ALU.add,
            )
            hid_codes = keep.tile([P, POINTS], U32, name="hid_codes%d" % rh, align_bytes=64)
            hid_plane = keep.tile([P, POINTS], U8, name="hid_plane%d" % rh, align_bytes=64)
            nc.vector.quantize_mx(hid_codes[:].bitcast(FP8X4), hid_plane[:], hid[:])
            result = keep.tile([P, N // P, POINTS], F32, name="result%d" % rh)
            for mt in range(N // P):
                bank = psum.tile([P, POINTS], F32, name="bank%d" % out_banks[rh][mt])
                nc.tensor.matmul_mx(
                    out=bank[:],
                    lhsT=codes3[:, mt * P : (mt + 1) * P].bitcast(FP8X4),
                    lhsT_scale=plane3[:, mt * P : (mt + 1) * P],
                    rhs=hid_codes[:].bitcast(FP8X4),
                    rhs_scale=hid_plane[:],
                    start=True,
                    stop=True,
                )
                leave = on_v if (rh, mt) == (1, 1) else on_s
                leave(result[:, mt, :], bank[:])
            nc.sync.dma_start(out[:, r0:r1].rearrange("(mt p) r -> p mt r", p=P), result[:])
